import numpy as np
import ml_dtypes


def mxq(x, axis, fmt="e4m3"):
    dtype, down = {"e4m3": (ml_dtypes.float8_e4m3fn, 7), "e5m2": (ml_dtypes.float8_e5m2, 14)}[fmt]
    v = np.moveaxis(np.asarray(x, np.float32).astype(ml_dtypes.bfloat16).astype(np.float64), axis, -1)
    blocks = v.reshape(v.shape[:-1] + (-1, 32))
    amax = np.abs(blocks).max(-1, keepdims=True)
    byte = np.maximum(np.where(amax > 0, np.frexp(amax)[1] - 1 + 127, 0) - down, 1)
    scale = np.exp2(byte - 127.0)
    codes = (blocks / scale).astype(np.float32).astype(dtype).astype(np.float64)
    return np.moveaxis((codes * scale).reshape(v.shape), -1, axis)


WIDE = False


def mx_kscale(k):
    if not WIDE:
        return np.ones(k)
    levels = np.array([10, -10, 5, -5, 0])
    if k % 512:
        return np.exp2(np.random.permutation(np.resize(levels, k // 32))).repeat(32)
    a = np.empty((k // 512, 16))
    for p in range(k // 512):
        a[p, :8] = np.random.permutation(np.resize(levels, 8))
        for g in range(8):
            far = levels[np.abs(levels - a[p, g]) >= 10]
            a[p, g + 8] = far[np.random.randint(len(far))]
    return np.exp2(a.ravel()).repeat(32)


def f64(x):
    return np.asarray(x).astype(np.float64)


def striped(idx):
    return np.tile(idx.reshape(-1, 16).T, (8, 1)).astype(np.uint16)


def unstriped(offs):
    return offs[:16].T.reshape(-1).astype(np.int64)


def pack_weight(w):
    k, n = w.shape
    w = f64(np.asarray(w, np.float32).astype(ml_dtypes.bfloat16)).reshape(k // 32, 32, n)
    amax = np.abs(w).max(1)
    byte = np.clip(np.where(amax > 0, np.frexp(amax)[1] - 1 + 127 - 7, 1), 1, 254)
    scaled = (w * np.exp2(127.0 - byte)[:, None, :]).reshape(k, n).astype(np.float32)
    words = np.ascontiguousarray(scaled.reshape(k // 512, 128, 4, n).transpose(0, 1, 3, 2)).astype(ml_dtypes.float8_e4m3fn).view(np.uint8)
    return words, np.ascontiguousarray(byte.astype(np.uint8).reshape(k // 512, 16, n))


def unpack_weight(words, scales):
    g, p, n, _ = words.shape
    vals = np.ascontiguousarray(words).view(ml_dtypes.float8_e4m3fn).astype(np.float64) * np.repeat(np.exp2(scales.astype(np.float64) - 127.0), 8, axis=1)[..., None]
    return vals.transpose(0, 1, 3, 2).reshape(g * 512, n)


def relu2(v):
    return np.maximum(v, 0.0) ** 2


K, T, D, S, V, R, N = 2048, 1024, 4, 1024, 256, 4, 128


def setup_inputs():
    n = np.random.standard_normal
    s = mx_kscale(K)[:, None]
    packed = pack_weight(n((K, T)) * s)
    return {
        "x_words": packed[0],
        "x_scales": packed[1],
        "w": (n((D, K, N)) / np.sqrt(D * K) / s[None]).astype(np.float32),
        "b": (0.3 * n((N, 1))).astype(np.float32),
        "offs": striped(np.concatenate([R * np.arange(V) + np.random.randint(0, R, V) for _ in range(D)])),
    }


def reference(x_words, x_scales, w, b, offs):
    idx = unstriped(offs)
    xq = unpack_weight(x_words, x_scales)[:, idx]
    wq = mxq(f64(w), 1, "e4m3")
    y = sum(wq[d].T @ xq[:, d * V:(d + 1) * V] for d in range(D))
    y = relu2(y + f64(b))
    return y

@@ -1,0 +1,116 @@
+from contextlib import ExitStack
+
+import concourse.mybir as mybir
+
+K, T, D, V, N = 2048, 1024, 4, 256, 128
+S = D * V
+FLOPS = 2 * D * K * N * V
+
+F32 = mybir.dt.float32
+BF16 = mybir.dt.bfloat16
+I32 = mybir.dt.int32
+U32 = mybir.dt.uint32
+U16 = mybir.dt.uint16
+U8 = mybir.dt.uint8
+FP8X4 = mybir.dt.float8_e4m3fn_x4
+ALU = mybir.AluOpType
+
+P = 128
+PACK = 4
+K_PASS = P * PACK
+PASSES = K // K_PASS
+STRIPE = 16
+GATHER = 512
+RUN = 4
+
+
+def tile_picked_deform_lin_relu2_def_p_kernel(tc, x_words, x_scales, w, b, offs, out):
+    nc = tc.nc
+    with ExitStack() as ctx:
+        pool = ctx.enter_context(tc.tile_pool(name="held", bufs=1))
+        psum = ctx.enter_context(tc.psum_pool(name="psum", bufs=1))
+
+        offsets = pool.tile([P, S // STRIPE], U16, name="offsets")
+        nc.sync.dma_start(offsets[:], offs)
+
+        scale_table = pool.tile([P, T], U8, name="scale_table", align_bytes=64)
+        nc.vector.memset(scale_table[:].bitcast(I32), 0)
+        for q in range(4):
+            nc.scalar.dma_start(
+                out=scale_table[32 * q : 32 * q + 16, :].bitcast(I32),
+                in_=x_scales.bitcast(I32)[:, 4 * q : 4 * q + 4, :],
+            )
+        bias = pool.tile([P, 1], F32, name="bias")
+        nc.scalar.dma_start(out=bias[:], in_=b)
+
+        word_tables = {}
+        raw = {}
+
+        def load_x(o):
+            word_tables[o] = pool.tile([P, T], U32, name="word_table%d" % o, align_bytes=64)
+            nc.sync.dma_start(
+                out=word_tables[o][:].bitcast(I32),
+                in_=x_words[o].rearrange("p c r -> p (c r)").bitcast(I32),
+            )
+
+        def load_w(o, d):
+            raw[o, d] = pool.tile([P, PACK, N], F32, name="raw%d_%d" % (o, d), align_bytes=64)
+            nc.sync.dma_start(
+                out=raw[o, d][:],
+                in_=w[d, o * K_PASS : (o + 1) * K_PASS, :].rearrange("(p t) m -> p t m", t=PACK),
+            )
+
+        chunks = [(o, d) for o in range(PASSES) for d in range(D)]
+        for o in range(PASSES):
+            load_x(o)
+            for c in chunks[2 * o : 2 * o + 2]:
+                load_w(*c)
+        for c in chunks[2 * PASSES :]:
+            load_w(*c)
+
+        def gather(dst, table):
+            for j in range(0, S, GATHER):
+                nc.vector.tensor_copy(
+                    dst[:, j : j + GATHER],
+                    table[:].indirect(offsets[:, j // STRIPE : (j + GATHER) // STRIPE]),
+                )
+
+        picked_scales = pool.tile([P, S], U8, name="picked_scales", align_bytes=64)
+        gather(picked_scales, scale_table)
+
+        acc = psum.tile([N, V], F32, name="acc")
+        picked = {}
+        for o, d in chunks:
+            if d == 0:
+                picked[o] = pool.tile([P, S], U32, name="picked%d" % o, align_bytes=64)
+                gather(picked[o], word_tables[o])
+            grouped = pool.tile([P, N, PACK], BF16, name="grouped%d_%d" % (o, d), align_bytes=64)
+            dst = grouped[:].rearrange("p (c i) t -> p c t i", i=RUN)
+            src = raw[o, d][:].rearrange("p t (c i) -> p c t i", i=RUN)
+            if (o, d) == chunks[-1]:
+                nc.vector.tensor_copy(out=dst, in_=src)
+            else:
+                nc.scalar.copy(out=dst, in_=src)
+            codes = pool.tile([P, N], U32, name="codes%d_%d" % (o, d), align_bytes=64)
+            scales = pool.tile([P, N], U8, name="scales%d_%d" % (o, d), align_bytes=64)
+            nc.vector.quantize_mx(
+                out=codes[:].bitcast(FP8X4),
+                scales=scales[:],
+                in_=grouped[:].rearrange("p m t -> p (m t)"),
+            )
+            cols = slice(d * V, (d + 1) * V)
+            nc.tensor.matmul_mx(
+                out=acc[:],
+                lhsT=codes[:].bitcast(FP8X4),
+                lhsT_scale=scales[:],
+                rhs=picked[o][:, cols].bitcast(FP8X4),
+                rhs_scale=picked_scales[4 * o : P, cols],
+                start=((o, d) == chunks[0]),
+                stop=((o, d) == chunks[-1]),
+            )
+
+        relu = pool.tile([N, V], F32, name="relu")
+        nc.vector.tensor_scalar(relu[:], acc[:], bias[:], 0.0, ALU.add, ALU.max)
+        result = pool.tile([N, V], F32, name="result")
+        nc.vector.tensor_tensor(result[:], relu[:], relu[:], ALU.mult)
+        nc.sync.dma_start(out=out, in_=result[:])

@@ -19,8 +19,10 @@ P = 128
 PACK = 4
 K_PASS = P * PACK
 PASSES = K // K_PASS
+LAST = PASSES - 1
 STRIPE = 16
-GATHER = 512
+SPARE = 384
+WINDOW = T + SPARE
 RUN = 4
 
 
@@ -30,87 +32,108 @@ def tile_picked_deform_lin_relu2_def_p_kernel(tc, x_words, x_scales, w, b, offs,
         pool = ctx.enter_context(tc.tile_pool(name="held", bufs=1))
         psum = ctx.enter_context(tc.psum_pool(name="psum", bufs=1))
 
-        offsets = pool.tile([P, S // STRIPE], U16, name="offsets")
-        nc.sync.dma_start(offsets[:], offs)
-
-        scale_table = pool.tile([P, T], U8, name="scale_table", align_bytes=64)
-        nc.vector.memset(scale_table[:].bitcast(I32), 0)
-        for q in range(4):
-            nc.scalar.dma_start(
-                out=scale_table[32 * q : 32 * q + 16, :].bitcast(I32),
-                in_=x_scales.bitcast(I32)[:, 4 * q : 4 * q + 4, :],
-            )
-        bias = pool.tile([P, 1], F32, name="bias")
-        nc.scalar.dma_start(out=bias[:], in_=b)
-
-        word_tables = {}
+        word_table = pool.tile([P, PASSES * T + SPARE], U32, name="word_table", align_bytes=64)
         raw = {}
 
-        def load_x(o):
-            word_tables[o] = pool.tile([P, T], U32, name="word_table%d" % o, align_bytes=64)
+        def base(o):
+            return (LAST - o) * T
+
+        def load_x(o, c0, c1):
             nc.sync.dma_start(
-                out=word_tables[o][:].bitcast(I32),
-                in_=x_words[o].rearrange("p c r -> p (c r)").bitcast(I32),
+                out=word_table[:, base(o) + c0 : base(o) + c1].bitcast(I32),
+                in_=x_words[o].rearrange("p c r -> p (c r)").bitcast(I32)[:, c0:c1],
             )
 
         def load_w(o, d):
-            raw[o, d] = pool.tile([P, PACK, N], F32, name="raw%d_%d" % (o, d), align_bytes=64)
+            raw[o, d] = pool.tile([P, PACK, N], F32, name="raw%d_%d" % (o, d), tag="raw%d_%d" % (o, d), align_bytes=64)
             nc.sync.dma_start(
                 out=raw[o, d][:],
                 in_=w[d, o * K_PASS : (o + 1) * K_PASS, :].rearrange("(p t) m -> p t m", t=PACK),
             )
 
+        load_x(0, 0, T // 2)
+        offsets = pool.tile([P, S // STRIPE], U16, name="offsets")
+        nc.sync.dma_start(offsets[:], offs)
+        load_x(0, T // 2, T)
+
+        scale_table = pool.tile([P, WINDOW], U8, name="scale_table", align_bytes=64)
+        nc.vector.memset(scale_table[:].bitcast(I32), 0)
+        nc.vector.memset(word_table[:, PASSES * T :].bitcast(I32), 0)
+        for q in range(4):
+            nc.sync.dma_start(
+                out=scale_table[32 * q : 32 * q + 16, 0:T].bitcast(I32),
+                in_=x_scales.bitcast(I32)[:, 4 * q : 4 * q + 4, :],
+            )
+        bias = pool.tile([P, 1], F32, name="bias")
+
         chunks = [(o, d) for o in range(PASSES) for d in range(D)]
-        for o in range(PASSES):
-            load_x(o)
-            for c in chunks[2 * o : 2 * o + 2]:
+        for o in range(1, PASSES):
+            for c in chunks[3 * (o - 1) : 3 * o]:
                 load_w(*c)
-        for c in chunks[2 * PASSES :]:
+            load_x(o, 0, T)
+        nc.sync.dma_start(out=bias[:], in_=b)
+        for c in chunks[3 * (PASSES - 1) :]:
             load_w(*c)
 
-        def gather(dst, table):
-            for j in range(0, S, GATHER):
-                nc.vector.tensor_copy(
-                    dst[:, j : j + GATHER],
-                    table[:].indirect(offsets[:, j // STRIPE : (j + GATHER) // STRIPE]),
-                )
+        def gather(dst, window, j0, j1):
+            nc.vector.tensor_copy(dst, window.indirect(offsets[:, j0 // STRIPE : j1 // STRIPE]))
+
+        def words_of(o, width):
+            return word_table[:, base(o) : base(o) + width]
+
+        picked = [pool.tile([P, S], U32, name="picked%d" % o, align_bytes=64) for o in range(LAST)]
+        gather(picked[0][:, 0 : V // 2], words_of(0, T // 2), 0, V // 2)
+        gather(picked[0][:, V // 2 : S], words_of(0, WINDOW), V // 2, S)
 
         picked_scales = pool.tile([P, S], U8, name="picked_scales", align_bytes=64)
-        gather(picked_scales, scale_table)
+        gather(picked_scales[:], scale_table[:], 0, S)
 
         acc = psum.tile([N, V], F32, name="acc")
-        picked = {}
-        for o, d in chunks:
-            if d == 0:
-                picked[o] = pool.tile([P, S], U32, name="picked%d" % o, align_bytes=64)
-                gather(picked[o], word_tables[o])
-            grouped = pool.tile([P, N, PACK], BF16, name="grouped%d_%d" % (o, d), align_bytes=64)
-            dst = grouped[:].rearrange("p (c i) t -> p c t i", i=RUN)
-            src = raw[o, d][:].rearrange("p t (c i) -> p c t i", i=RUN)
-            if (o, d) == chunks[-1]:
-                nc.vector.tensor_copy(out=dst, in_=src)
-            else:
-                nc.scalar.copy(out=dst, in_=src)
-            codes = pool.tile([P, N], U32, name="codes%d_%d" % (o, d), align_bytes=64)
-            scales = pool.tile([P, N], U8, name="scales%d_%d" % (o, d), align_bytes=64)
-            nc.vector.quantize_mx(
-                out=codes[:].bitcast(FP8X4),
-                scales=scales[:],
-                in_=grouped[:].rearrange("p m t -> p (m t)"),
-            )
-            cols = slice(d * V, (d + 1) * V)
-            nc.tensor.matmul_mx(
-                out=acc[:],
-                lhsT=codes[:].bitcast(FP8X4),
-                lhsT_scale=scales[:],
-                rhs=picked[o][:, cols].bitcast(FP8X4),
-                rhs_scale=picked_scales[4 * o : P, cols],
-                start=((o, d) == chunks[0]),
-                stop=((o, d) == chunks[-1]),
-            )
 
-        relu = pool.tile([N, V], F32, name="relu")
-        nc.vector.tensor_scalar(relu[:], acc[:], bias[:], 0.0, ALU.add, ALU.max)
-        result = pool.tile([N, V], F32, name="result")
-        nc.vector.tensor_tensor(result[:], relu[:], relu[:], ALU.mult)
-        nc.sync.dma_start(out=out, in_=result[:])
+        def product(o, taps, rhs_of):
+            grouped = pool.tile([P, len(taps), N, PACK], BF16, name="grouped%d_%d" % (o, taps[0]), align_bytes=64)
+            codes = pool.tile([P, len(taps), N], U32, name="codes%d_%d" % (o, taps[0]), align_bytes=64)
+            scales = pool.tile([P, len(taps), N], U8, name="scales%d_%d" % (o, taps[0]), align_bytes=64)
+            for i, d in enumerate(taps):
+                nc.scalar.copy(
+                    out=grouped[:, i].rearrange("p (c i) t -> p c t i", i=RUN),
+                    in_=raw[o, d][:].rearrange("p t (c i) -> p c t i", i=RUN),
+                )
+            nc.vector.quantize_mx(
+                out=codes[:].rearrange("p d m -> p (d m)").bitcast(FP8X4),
+                scales=scales[:].rearrange("p d m -> p (d m)"),
+                in_=grouped[:].rearrange("p d m t -> p (d m t)"),
+            )
+            for i, d in enumerate(taps):
+                nc.tensor.matmul_mx(
+                    out=acc[:],
+                    lhsT=codes[:, i].bitcast(FP8X4),
+                    lhsT_scale=scales[:, i],
+                    rhs=rhs_of(d).bitcast(FP8X4),
+                    rhs_scale=picked_scales[4 * o : P, d * V : (d + 1) * V],
+                    start=((o, d) == chunks[0]),
+                    stop=((o, d) == chunks[-1]),
+                )
+
+        for o in range(LAST):
+            if o > 0:
+                gather(picked[o][:], words_of(o, WINDOW), 0, S)
+            product(o, list(range(D)), lambda d: picked[o][:, d * V : (d + 1) * V])
+
+        half = S // 2
+        early = pool.tile([P, half], U32, name="picked_early", align_bytes=64)
+        gather(early[:], words_of(LAST, T), 0, half)
+        for d in range(D // 2):
+            product(LAST, [d], lambda d: early[:, d * V : (d + 1) * V])
+        late = pool.tile([P, half], U32, name="picked_late", tag="raw%d_%d" % (LAST, 1), align_bytes=64)
+        gather(late[:], words_of(LAST, T), half, S)
+        for d in range(D // 2, D):
+            product(LAST, [d], lambda d: late[:, d * V - half : (d + 1) * V - half])
+
+        for h, queue in enumerate((nc.sync, nc.scalar)):
+            cols = slice(h * V // 2, (h + 1) * V // 2)
+            relu = pool.tile([N, V // 2], F32, name="relu%d" % h)
+            nc.scalar.activation(relu[:], acc[:, cols], mybir.ActivationFunctionType.Relu, bias=bias[:])
+            result = pool.tile([N, V // 2], F32, name="result%d" % h)
+            nc.vector.tensor_tensor(result[:], relu[:], relu[:], ALU.mult)
+            queue.dma_start(out=out[:, cols], in_=result[:])

@@ -44,12 +44,14 @@ def tile_picked_deform_lin_relu2_def_p_kernel(tc, x_words, x_scales, w, b, offs,
                 in_=x_words[o].rearrange("p c r -> p (c r)").bitcast(I32)[:, c0:c1],
             )
 
-        def load_w(o, d):
-            raw[o, d] = pool.tile([P, PACK, N], F32, name="raw%d_%d" % (o, d), tag="raw%d_%d" % (o, d), align_bytes=64)
+        def load_w(o, d0, d1):
+            tile = pool.tile([P, d1 - d0, PACK, N], F32, name="raw%d_%d" % (o, d0), align_bytes=64)
             nc.sync.dma_start(
-                out=raw[o, d][:],
-                in_=w[d, o * K_PASS : (o + 1) * K_PASS, :].rearrange("(p t) m -> p t m", t=PACK),
+                out=tile[:].rearrange("p d t m -> p d (t m)"),
+                in_=w[d0:d1, o * K_PASS : (o + 1) * K_PASS, :].rearrange("d (p t) m -> p d (t m)", t=PACK),
             )
+            for d in range(d0, d1):
+                raw[o, d] = tile[:, d - d0]
 
         load_x(0, 0, T // 2)
         offsets = pool.tile([P, S // STRIPE], U16, name="offsets")
@@ -67,13 +69,15 @@ def tile_picked_deform_lin_relu2_def_p_kernel(tc, x_words, x_scales, w, b, offs,
         bias = pool.tile([P, 1], F32, name="bias")
 
         chunks = [(o, d) for o in range(PASSES) for d in range(D)]
+        pairs = [(o, d, d + 2) for o in range(LAST) for d in (0, 2)]
         for o in range(1, PASSES):
-            for c in chunks[3 * (o - 1) : 3 * o]:
-                load_w(*c)
+            load_w(*pairs[o - 1])
             load_x(o, 0, T)
         nc.sync.dma_start(out=bias[:], in_=b)
-        for c in chunks[3 * (PASSES - 1) :]:
-            load_w(*c)
+        for pair in pairs[LAST:]:
+            load_w(*pair)
+        for d in range(D):
+            load_w(LAST, d, d + 1)
 
         def gather(dst, window, j0, j1):
             nc.vector.tensor_copy(dst, window.indirect(offsets[:, j0 // STRIPE : j1 // STRIPE]))
@@ -81,7 +85,7 @@ def tile_picked_deform_lin_relu2_def_p_kernel(tc, x_words, x_scales, w, b, offs,
         def words_of(o, width):
             return word_table[:, base(o) : base(o) + width]
 
-        picked = [pool.tile([P, S], U32, name="picked%d" % o, align_bytes=64) for o in range(LAST)]
+        picked = [pool.tile([P, S], U32, name="picked%d" % o, align_bytes=64) for o in range(PASSES)]
         gather(picked[0][:, 0 : V // 2], words_of(0, T // 2), 0, V // 2)
         gather(picked[0][:, V // 2 : S], words_of(0, WINDOW), V // 2, S)
 
@@ -90,14 +94,14 @@ def tile_picked_deform_lin_relu2_def_p_kernel(tc, x_words, x_scales, w, b, offs,
 
         acc = psum.tile([N, V], F32, name="acc")
 
-        def product(o, taps, rhs_of):
+        def product(o, taps, interleave):
             grouped = pool.tile([P, len(taps), N, PACK], BF16, name="grouped%d_%d" % (o, taps[0]), align_bytes=64)
             codes = pool.tile([P, len(taps), N], U32, name="codes%d_%d" % (o, taps[0]), align_bytes=64)
             scales = pool.tile([P, len(taps), N], U8, name="scales%d_%d" % (o, taps[0]), align_bytes=64)
             for i, d in enumerate(taps):
-                nc.scalar.copy(
+                interleave(
                     out=grouped[:, i].rearrange("p (c i) t -> p c t i", i=RUN),
-                    in_=raw[o, d][:].rearrange("p t (c i) -> p c t i", i=RUN),
+                    in_=raw[o, d].rearrange("p t (c i) -> p c t i", i=RUN),
                 )
             nc.vector.quantize_mx(
                 out=codes[:].rearrange("p d m -> p (d m)").bitcast(FP8X4),
@@ -109,26 +113,19 @@ def tile_picked_deform_lin_relu2_def_p_kernel(tc, x_words, x_scales, w, b, offs,
                     out=acc[:],
                     lhsT=codes[:, i].bitcast(FP8X4),
                     lhsT_scale=scales[:, i],
-                    rhs=rhs_of(d).bitcast(FP8X4),
+                    rhs=picked[o][:, d * V : (d + 1) * V].bitcast(FP8X4),
                     rhs_scale=picked_scales[4 * o : P, d * V : (d + 1) * V],
                     start=((o, d) == chunks[0]),
                     stop=((o, d) == chunks[-1]),
                 )
 
-        for o in range(LAST):
+        for o in range(PASSES):
             if o > 0:
                 gather(picked[o][:], words_of(o, WINDOW), 0, S)
-            product(o, list(range(D)), lambda d: picked[o][:, d * V : (d + 1) * V])
-
-        half = S // 2
-        early = pool.tile([P, half], U32, name="picked_early", align_bytes=64)
-        gather(early[:], words_of(LAST, T), 0, half)
-        for d in range(D // 2):
-            product(LAST, [d], lambda d: early[:, d * V : (d + 1) * V])
-        late = pool.tile([P, half], U32, name="picked_late", tag="raw%d_%d" % (LAST, 1), align_bytes=64)
-        gather(late[:], words_of(LAST, T), half, S)
-        for d in range(D // 2, D):
-            product(LAST, [d], lambda d: late[:, d * V - half : (d + 1) * V - half])
+            if o < LAST:
+                product(o, list(range(D)), nc.scalar.copy)
+        for d in range(D):
+            product(LAST, [d], nc.vector.tensor_copy if d % 2 else nc.scalar.copy)
 
         for h, queue in enumerate((nc.sync, nc.scalar)):
             cols = slice(h * V // 2, (h + 1) * V // 2)

from contextlib import ExitStack

import concourse.mybir as mybir

K, T, D, V, N = 2048, 1024, 4, 256, 128
S = D * V
FLOPS = 2 * D * K * N * V

F32 = mybir.dt.float32
BF16 = mybir.dt.bfloat16
I32 = mybir.dt.int32
U32 = mybir.dt.uint32
U16 = mybir.dt.uint16
U8 = mybir.dt.uint8
FP8X4 = mybir.dt.float8_e4m3fn_x4
ALU = mybir.AluOpType

P = 128
PACK = 4
K_PASS = P * PACK
PASSES = K // K_PASS
LAST = PASSES - 1
STRIPE = 16
SPARE = 384
WINDOW = T + SPARE
RUN = 4


def tile_picked_deform_lin_relu2_def_p_kernel(tc, x_words, x_scales, w, b, offs, out):
    nc = tc.nc
    with ExitStack() as ctx:
        pool = ctx.enter_context(tc.tile_pool(name="held", bufs=1))
        psum = ctx.enter_context(tc.psum_pool(name="psum", bufs=1))

        word_table = pool.tile([P, PASSES * T + SPARE], U32, name="word_table", align_bytes=64)
        raw = {}

        def base(o):
            return (LAST - o) * T

        def load_x(o, c0, c1):
            nc.sync.dma_start(
                out=word_table[:, base(o) + c0 : base(o) + c1].bitcast(I32),
                in_=x_words[o].rearrange("p c r -> p (c r)").bitcast(I32)[:, c0:c1],
            )

        def load_w(o, d0, d1):
            tile = pool.tile([P, d1 - d0, PACK, N], F32, name="raw%d_%d" % (o, d0), align_bytes=64)
            nc.sync.dma_start(
                out=tile[:].rearrange("p d t m -> p d (t m)"),
                in_=w[d0:d1, o * K_PASS : (o + 1) * K_PASS, :].rearrange("d (p t) m -> p d (t m)", t=PACK),
            )
            for d in range(d0, d1):
                raw[o, d] = tile[:, d - d0]

        load_x(0, 0, T // 2)
        offsets = pool.tile([P, S // STRIPE], U16, name="offsets")
        nc.sync.dma_start(offsets[:], offs)
        load_x(0, T // 2, T)

        scale_table = pool.tile([P, WINDOW], U8, name="scale_table", align_bytes=64)
        nc.vector.memset(scale_table[:].bitcast(I32), 0)
        nc.vector.memset(word_table[:, PASSES * T :].bitcast(I32), 0)
        for q in range(4):
            nc.sync.dma_start(
                out=scale_table[32 * q : 32 * q + 16, 0:T].bitcast(I32),
                in_=x_scales.bitcast(I32)[:, 4 * q : 4 * q + 4, :],
            )
        bias = pool.tile([P, 1], F32, name="bias")

        chunks = [(o, d) for o in range(PASSES) for d in range(D)]
        pairs = [(o, d, d + 2) for o in range(LAST) for d in (0, 2)]
        for o in range(1, PASSES):
            load_w(*pairs[o - 1])
            load_x(o, 0, T)
        nc.sync.dma_start(out=bias[:], in_=b)
        for pair in pairs[LAST:]:
            load_w(*pair)
        for d in range(D):
            load_w(LAST, d, d + 1)

        def gather(dst, window, j0, j1):
            nc.vector.tensor_copy(dst, window.indirect(offsets[:, j0 // STRIPE : j1 // STRIPE]))

        def words_of(o, width):
            return word_table[:, base(o) : base(o) + width]

        picked = [pool.tile([P, S], U32, name="picked%d" % o, align_bytes=64) for o in range(PASSES)]
        gather(picked[0][:, 0 : V // 2], words_of(0, T // 2), 0, V // 2)
        gather(picked[0][:, V // 2 : S], words_of(0, WINDOW), V // 2, S)

        picked_scales = pool.tile([P, S], U8, name="picked_scales", align_bytes=64)
        gather(picked_scales[:], scale_table[:], 0, S)

        acc = psum.tile([N, V], F32, name="acc")

        def product(o, taps, interleave):
            grouped = pool.tile([P, len(taps), N, PACK], BF16, name="grouped%d_%d" % (o, taps[0]), align_bytes=64)
            codes = pool.tile([P, len(taps), N], U32, name="codes%d_%d" % (o, taps[0]), align_bytes=64)
            scales = pool.tile([P, len(taps), N], U8, name="scales%d_%d" % (o, taps[0]), align_bytes=64)
            for i, d in enumerate(taps):
                interleave(
                    out=grouped[:, i].rearrange("p (c i) t -> p c t i", i=RUN),
                    in_=raw[o, d].rearrange("p t (c i) -> p c t i", i=RUN),
                )
            nc.vector.quantize_mx(
                out=codes[:].rearrange("p d m -> p (d m)").bitcast(FP8X4),
                scales=scales[:].rearrange("p d m -> p (d m)"),
                in_=grouped[:].rearrange("p d m t -> p (d m t)"),
            )
            for i, d in enumerate(taps):
                nc.tensor.matmul_mx(
                    out=acc[:],
                    lhsT=codes[:, i].bitcast(FP8X4),
                    lhsT_scale=scales[:, i],
                    rhs=picked[o][:, d * V : (d + 1) * V].bitcast(FP8X4),
                    rhs_scale=picked_scales[4 * o : P, d * V : (d + 1) * V],
                    start=((o, d) == chunks[0]),
                    stop=((o, d) == chunks[-1]),
                )

        for o in range(PASSES):
            if o > 0:
                gather(picked[o][:], words_of(o, WINDOW), 0, S)
            if o < LAST:
                product(o, list(range(D)), nc.scalar.copy)
        for d in range(D):
            product(LAST, [d], nc.vector.tensor_copy if d % 2 else nc.scalar.copy)

        for h, queue in enumerate((nc.sync, nc.scalar)):
            cols = slice(h * V // 2, (h + 1) * V // 2)
            relu = pool.tile([N, V // 2], F32, name="relu%d" % h)
            nc.scalar.activation(relu[:], acc[:, cols], mybir.ActivationFunctionType.Relu, bias=bias[:])
            result = pool.tile([N, V // 2], F32, name="result%d" % h)
            nc.vector.tensor_tensor(result[:], relu[:], relu[:], ALU.mult)
            queue.dma_start(out=out[:, cols], in_=result[:])
